import numpy as np
import ml_dtypes


def mxq(x, axis, fmt="e4m3"):
    dtype, down = {"e4m3": (ml_dtypes.float8_e4m3fn, 7), "e5m2": (ml_dtypes.float8_e5m2, 14)}[fmt]
    v = np.moveaxis(np.asarray(x, np.float32).astype(ml_dtypes.bfloat16).astype(np.float64), axis, -1)
    blocks = v.reshape(v.shape[:-1] + (-1, 32))
    amax = np.abs(blocks).max(-1, keepdims=True)
    byte = np.maximum(np.where(amax > 0, np.frexp(amax)[1] - 1 + 127, 0) - down, 1)
    scale = np.exp2(byte - 127.0)
    codes = (blocks / scale).astype(np.float32).astype(dtype).astype(np.float64)
    return np.moveaxis((codes * scale).reshape(v.shape), -1, axis)


WIDE = False


def mx_kscale(k):
    if not WIDE:
        return np.ones(k)
    levels = np.array([30, -30])
    if k % 512:
        return np.exp2(np.random.permutation(np.resize(levels, k // 32))).repeat(32)
    a = np.empty((k // 512, 16))
    for p in range(k // 512):
        a[p, :8] = np.random.permutation(np.resize(levels, 8))
        for g in range(8):
            far = levels[np.abs(levels - a[p, g]) >= 10]
            a[p, g + 8] = far[np.random.randint(len(far))]
    return np.exp2(a.ravel()).repeat(32)


BF16 = ml_dtypes.bfloat16


def bf(x):
    return np.asarray(x, np.float32).astype(BF16)


def f64(x):
    return np.asarray(x).astype(np.float64)


E2M1 = np.array([0.0, 0.5, 1.0, 1.5, 2.0, 3.0, 4.0, 6.0, -0.0, -0.5, -1.0, -1.5, -2.0, -3.0, -4.0, -6.0])


def pack_weight(w, fmt):
    k, n = w.shape
    w = f64(bf(w)).reshape(k // 32, 32, n)
    amax = np.abs(w).max(1)
    if fmt in ("e4m3", "e5m2"):
        byte = np.frexp(amax)[1] - 1 + 127 - (7 if fmt == "e4m3" else 14)
    else:
        mant, ex = np.frexp(amax / 6.0)
        byte = np.where(mant > 0.5, ex, ex - 1) + 127
    byte = np.clip(np.where(amax > 0, byte, 1), 1, 254)
    scaled = (w * np.exp2(127.0 - byte)[:, None, :]).reshape(k, n).astype(np.float32)
    by_word = np.ascontiguousarray(scaled.reshape(k // 512, 128, 4, n).transpose(0, 1, 3, 2))
    if fmt in ("e4m3", "e5m2"):
        words = by_word.astype(ml_dtypes.float8_e4m3fn if fmt == "e4m3" else ml_dtypes.float8_e5m2).view(np.uint8)
    else:
        c = by_word.astype(ml_dtypes.float4_e2m1fn).view(np.uint8) & 0xF
        words = c[..., 0::2] | (c[..., 1::2] << 4)
    return np.ascontiguousarray(words), np.ascontiguousarray(byte.astype(np.uint8).reshape(k // 512, 16, n))


def unpack_weight(words, scales, fmt):
    g, p, n, _ = words.shape
    if fmt in ("e4m3", "e5m2"):
        vals = np.ascontiguousarray(words).view(ml_dtypes.float8_e4m3fn if fmt == "e4m3" else ml_dtypes.float8_e5m2).astype(np.float64)
    else:
        nib = np.empty((g, p, n, 4), np.uint8)
        nib[..., 0::2] = words & 0xF
        nib[..., 1::2] = words >> 4
        vals = E2M1[nib]
    vals = vals * np.repeat(np.exp2(scales.astype(np.float64) - 127.0), 8, axis=1)[..., None]
    return vals.transpose(0, 1, 3, 2).reshape(g * 512, n)

def planes(Y):
    n, m = Y.shape
    b = f64(bf(Y)).reshape(n // 32, 32, m)
    amax = np.abs(b).max(1)
    byte = np.clip(np.where(amax > 0, np.frexp(amax)[1] - 1 + 127 - 7, 1), 1, 254)
    codes = (b * np.exp2(127.0 - byte)[:, None, :]).reshape(n, m).astype(np.float32).astype(ml_dtypes.float8_e4m3fn).view(np.uint8)
    words = codes.reshape(n // 512, 128, 4, m).transpose(0, 1, 3, 2)
    return np.ascontiguousarray(words), np.ascontiguousarray(byte.astype(np.uint8).reshape(n // 512, 16, m))


T, S, D = 1536, 1024, 1024
CAP = 4.0


def setup_inputs():
    logits = 1.6 * np.random.randn(1, S) + 1.6 * np.random.randn(T, S)
    th = np.tanh(logits / CAP)
    e = np.exp(CAP * (th - th.max(axis=1, keepdims=True)))
    A = e / e.sum(axis=1, keepdims=True)
    V = (np.random.randn(S, D) + 0.5 * np.random.randn(1, D)).astype(np.float32)
    G = (np.random.randn(T, D) * np.exp(np.random.randn(T, D)) / np.sqrt(D)).astype(np.float32)
    delta = np.array([(a * (V * g).sum(axis=1)).sum() for a, g in zip(A, G)])
    sc = mx_kscale(D)
    g_words, g_scales = pack_weight(f64(G).T / sc[:, None], "e5m2")
    return {
        "g_words": g_words,
        "g_scales": g_scales,
        "v": bf(V * sc),
        "weights": bf(S * A),
        "slope": bf(1.0 - th * th),
        "delta": bf(delta),
    }


def reference(g_words, g_scales, v, weights, slope, delta):
    GT = unpack_weight(g_words, g_scales, "e5m2")
    Vq = mxq(f64(v), 1, "e4m3")
    dA = GT.T @ Vq.T
    dB = f64(weights) * (dA - f64(delta)[:, None])
    y = dB * f64(slope)
    Y = y.T
    words, scales = planes(Y)
    return y, words, scales

@@ -1,0 +1,299 @@
+from contextlib import ExitStack
+
+import concourse.mybir as mybir
+from concourse.masks import make_identity
+
+T, S, D = 1536, 1024, 1024
+FLOPS = 2 * T * S * D
+
+F32 = mybir.dt.float32
+BF16 = mybir.dt.bfloat16
+I32 = mybir.dt.int32
+U32 = mybir.dt.uint32
+U8 = mybir.dt.uint8
+E4M3X4 = mybir.dt.float8_e4m3fn_x4
+E5M2X4 = mybir.dt.float8_e5m2_x4
+ALU = mybir.AluOpType
+
+P = 128
+HALF = 512
+N_TILES = T // P
+V_KEYS = 256
+
+
+def tile_softcap_logit_gradient_k2_kernel(
+    tc, g_words, g_scales, v, weights, slope, delta, out_0, out_1, out_2
+):
+    nc = tc.nc
+    with ExitStack() as ctx:
+        keep = ctx.enter_context(tc.tile_pool(name="keep", bufs=1))
+        ws_pool = ctx.enter_context(tc.tile_pool(name="ws_pool", bufs=2))
+        ybf_pool = ctx.enter_context(tc.tile_pool(name="ybf_pool", bufs=4))
+        grp_pool = ctx.enter_context(tc.tile_pool(name="grp_pool", bufs=3))
+        acc_pool = ctx.enter_context(tc.psum_pool(name="acc_pool", bufs=4))
+        turn_pool = ctx.enter_context(tc.psum_pool(name="turn_pool", bufs=4))
+        ctx.enter_context(tc.manual_schedule())
+
+        ident_f = keep.tile([P, P], F32, name="ident_f")
+        ident_b = keep.tile([P, P], BF16, name="ident_b")
+        delta_rows = keep.tile([P, P], BF16, name="delta_rows")
+        delta_col = keep.tile([P, N_TILES], F32, name="delta_col")
+        v_raw = keep.tile([P, 4, 2, D], BF16, name="v_raw", align_bytes=64)
+        v_grp = keep.tile([P, 4, 2, V_KEYS * 4], BF16, name="v_grp", align_bytes=64)
+        v_codes = keep.tile([P, 2, S], U32, name="v_codes", align_bytes=64)
+        v_scl = keep.tile([P, 2, S], U8, name="v_scl", align_bytes=64)
+        g_codes = keep.tile([P, 2, T], U32, name="g_codes", align_bytes=64)
+        g_scl = keep.tile([P, 2, T], U8, name="g_scl", align_bytes=64)
+        w_sb = keep.tile([P, N_TILES, S], BF16, name="w_sb", align_bytes=64)
+        s_sb = keep.tile([P, N_TILES, S], BF16, name="s_sb", align_bytes=64)
+        y_sb = keep.tile([P, N_TILES, S], F32, name="y_sb", align_bytes=64)
+        y_codes = keep.tile([P, 2, T], U32, name="y_codes", align_bytes=64)
+        y_scl = keep.tile([P, 2, T], U8, name="y_scl", align_bytes=64)
+
+        g_words_v = g_words.rearrange("g p n t -> p g (n t)")
+        out_words_v = out_1.rearrange("g p n t -> p g (n t)")
+        g_scales_v = g_scales.rearrange("g (q r) n -> r q g n", r=4)
+        out_scales_v = out_2.rearrange("g (q r) n -> r q g n", r=4)
+        w_v = weights.rearrange("(i p) s -> p i s", p=P)
+        s_v = slope.rearrange("(i p) s -> p i s", p=P)
+        y_v = out_0.rearrange("(i p) s -> p i s", p=P)
+
+        ws_head = keep.tile([P, 4, S], F32, name="ws_head", align_bytes=64)
+        shared = [keep.tile([P, 2, HALF], F32, name="shared%d" % r, align_bytes=64) for r in range(2)]
+        ws, acc, ybf, grp, ybank = {}, {}, {}, {}, {}
+
+        def load_v(c):
+            rows = v[c * V_KEYS : (c + 1) * V_KEYS, :]
+            nc.sync.dma_start(out=v_raw[:, c], in_=rows.rearrange("(p j) d -> p j d", j=2))
+
+        def load_g(n0, n1):
+            nc.sync.dma_start(
+                out=g_codes[:, :, n0:n1].bitcast(I32), in_=g_words_v[:, :, 4 * n0 : 4 * n1].bitcast(I32)
+            )
+
+        def load_ws(i0, i1):
+            nc.sync.dma_start(out=w_sb[:, i0:i1], in_=w_v[:, i0:i1])
+            nc.sync.dma_start(out=s_sb[:, i0:i1], in_=s_v[:, i0:i1])
+
+        def turn_v(c, g):
+            bank = turn_pool.tile([P, 2, 2, P], F32, name="bank")
+            for j in range(2):
+                words = v_raw[:, c, j, :].bitcast(F32)
+                for u in range(2):
+                    nc.tensor.transpose(bank[:, j, u, :], words[:, 256 * g + u : 256 * (g + 1) : 2], ident_f[:])
+            nc.scalar.copy(
+                out=v_grp[:, c, g, :].bitcast(F32).rearrange("k (m j u) -> k m j u", j=2, u=2),
+                in_=bank[:].rearrange("k j u m -> k m j u"),
+            )
+
+        def quant_v(c, g):
+            keys = slice(c * V_KEYS, (c + 1) * V_KEYS)
+            nc.vector.quantize_mx(
+                out=v_codes[:, g, keys].bitcast(E4M3X4), scales=v_scl[:, g, keys], in_=v_grp[:, c, g, :]
+            )
+
+        def product_tile(i):
+            nc.vector.tensor_tensor(out=ws_head[:, i, :], in0=w_sb[:, i, :], in1=s_sb[:, i, :], op=ALU.mult)
+            for h in range(2):
+                ws[i, h] = ws_head[:, i, h * HALF : (h + 1) * HALF]
+
+        def product_pair(engine, dst, pair, h):
+            tiles = slice(2 * pair, 2 * pair + 2)
+            keys = slice(h * HALF, (h + 1) * HALF)
+            engine.tensor_tensor(out=dst[:], in0=w_sb[:, tiles, keys], in1=s_sb[:, tiles, keys], op=ALU.mult)
+            for a in range(2):
+                ws[2 * pair + a, h] = dst[:, a, :]
+
+        def product_upper(pair):
+            dst = ws_pool.tile([P, 2, HALF], F32, name="ws")
+            product_pair(nc.vector, dst, pair, 1)
+
+        def product_lower(pair):
+            product_pair(nc.gpsimd, shared[pair % 2], pair, 0)
+
+        def matmul(i, h):
+            acc[i, h] = acc_pool.tile([P, HALF], F32, name="acc")
+            queries = slice(i * P, (i + 1) * P)
+            keys = slice(h * HALF, (h + 1) * HALF)
+            for g in range(2):
+                nc.tensor.matmul_mx(
+                    out=acc[i, h][:],
+                    lhsT=g_codes[:, g, queries].bitcast(E5M2X4),
+                    lhsT_scale=g_scl[:, g, queries],
+                    rhs=v_codes[:, g, keys].bitcast(E4M3X4),
+                    rhs_scale=v_scl[:, g, keys],
+                    start=(g == 0),
+                    stop=(g == 1),
+                )
+
+        def gradient(i, h):
+            keys = slice(h * HALF, (h + 1) * HALF)
+            nc.vector.scalar_tensor_tensor(
+                out=y_sb[:, i, keys],
+                in0=acc[i, h][:],
+                scalar=delta_col[:, i : i + 1],
+                in1=ws[i, h],
+                op0=ALU.subtract,
+                op1=ALU.mult,
+            )
+            ybf[i, h] = ybf_pool.tile([P, 2, P, 2], BF16, name="ybf")
+            nc.scalar.copy(
+                out=ybf[i, h][:], in_=y_sb[:, i, keys].rearrange("q (p u e) -> q u p e", u=2, e=2)
+            )
+
+        def turn_y(i0, n, h):
+            ybank[i0, h] = turn_pool.tile([P, n, 2, P], F32, name="bank")
+            for a in range(n):
+                for u in range(2):
+                    words = ybf[i0 + a, h][:, u].rearrange("q p e -> q (p e)").bitcast(F32)
+                    nc.tensor.transpose(ybank[i0, h][:, a, u, :], words, ident_f[:])
+
+        def group_y(i0, n, h, copy, home=None):
+            if home is None:
+                tile = grp_pool.tile([P, n * P * 2], F32, name="grp", align_bytes=64)
+                home = tile[:]
+            grp[i0, h] = home
+            copy(
+                out=home.rearrange("k (a m u) -> k a m u", a=n, u=2),
+                in_=ybank[i0, h][:].rearrange("k a u m -> k a m u"),
+            )
+
+        def quant_y(i0, n, h):
+            queries = slice(i0 * P, (i0 + n) * P)
+            nc.vector.quantize_mx(
+                out=y_codes[:, h, queries].bitcast(E4M3X4),
+                scales=y_scl[:, h, queries],
+                in_=grp[i0, h].bitcast(BF16),
+            )
+
+        def store_y(i0, i1, k0, k1):
+            nc.sync.dma_start(out=y_v[:, i0:i1, k0:k1], in_=y_sb[:, i0:i1, k0:k1])
+
+        def store_codes(h0, h1, n0, n1):
+            nc.sync.dma_start(
+                out=out_words_v[:, h0:h1, 4 * n0 : 4 * n1].bitcast(I32), in_=y_codes[:, h0:h1, n0:n1].bitcast(I32)
+            )
+
+        def store_scales(n0, n1, queues):
+            for r in range(4):
+                queues[r].dma_start(
+                    out=out_scales_v[r][:, :, n0:n1].bitcast(I32), in_=y_scl[r:P:32, :, n0:n1].bitcast(I32)
+                )
+
+        nc.vector.memset(g_scl[:].rearrange("p g n -> p (g n)").bitcast(I32), 0)
+        nc.vector.memset(delta_rows[:], 0.0)
+        make_identity(nc, ident_f[:])
+        for r in range(4):
+            nc.gpsimd.dma_start(out=g_scl[r:P:32].bitcast(I32), in_=g_scales_v[r].bitcast(I32))
+        nc.gpsimd.dma_start(out=delta_rows[0:N_TILES, :], in_=delta.rearrange("(i p) -> i p", p=P))
+        nc.vector.tensor_copy(out=ident_b[:], in_=ident_f[:])
+
+        load_v(0)
+        load_v(1)
+        load_ws(0, 1)
+        load_g(0, 256)
+        load_ws(1, 2)
+        load_ws(2, 3)
+        load_g(256, 512)
+        load_v(2)
+        load_ws(3, 4)
+        load_v(3)
+        load_ws(4, 6)
+        load_g(512, 1024)
+        load_ws(6, 8)
+        load_g(1024, 1536)
+        load_ws(8, 10)
+        load_ws(10, 12)
+
+        turn_v(0, 0)
+        turn_v(0, 1)
+        turn_v(1, 0)
+        turn_v(1, 1)
+        delta_bank = turn_pool.tile([P, P], BF16, name="bank")
+        nc.tensor.transpose(delta_bank[:], delta_rows[:], ident_b[:])
+        nc.scalar.copy(out=delta_col[:], in_=delta_bank[:, 0:N_TILES])
+        quant_v(0, 0)
+        quant_v(0, 1)
+        product_tile(0)
+        quant_v(1, 0)
+        quant_v(1, 1)
+        for i in range(4):
+            matmul(i, 0)
+        product_tile(1)
+        gradient(0, 0)
+        gradient(1, 0)
+        turn_v(2, 0)
+        turn_v(2, 1)
+        turn_y(0, 2, 0)
+        group_y(0, 2, 0, nc.scalar.copy)
+        product_tile(2)
+        gradient(2, 0)
+        product_tile(3)
+        quant_v(2, 0)
+        quant_v(2, 1)
+        turn_v(3, 0)
+        turn_v(3, 1)
+        gradient(3, 0)
+        quant_y(0, 2, 0)
+        quant_v(3, 0)
+        quant_v(3, 1)
+        turn_y(2, 2, 0)
+        matmul(0, 1)
+        matmul(1, 1)
+        matmul(2, 1)
+        matmul(3, 1)
+        group_y(2, 2, 0, nc.scalar.copy, shared[0][:, 0, :])
+        product_upper(2)
+        quant_y(2, 2, 0)
+
+        rounds = [[(0, 1), (2, 1)]] + [[(i0, 0), (i0, 1)] for i0 in range(4, N_TILES, 2)]
+        for n, (first, second) in enumerate(rounds):
+            last = n + 1 == len(rounds)
+            nxt = None if last else rounds[n + 1]
+            if not last:
+                product_lower(n + 2)
+            gradient(first[0], first[1])
+            gradient(first[0] + 1, first[1])
+            if last:
+                quant_y(rounds[n - 1][1][0], 2, 1)
+            if not last:
+                matmul(nxt[0][0], nxt[0][1])
+                matmul(nxt[0][0] + 1, nxt[0][1])
+            turn_y(first[0], 2, first[1])
+            gradient(second[0], second[1])
+            gradient(second[0] + 1, second[1])
+            if last:
+                break
+            matmul(nxt[1][0], nxt[1][1])
+            matmul(nxt[1][0] + 1, nxt[1][1])
+            turn_y(second[0], 2, second[1])
+            group_y(first[0], 2, first[1], nc.scalar.copy, shared[(n + 1) % 2][:, 0, :] if n + 3 < 6 else None)
+            group_y(second[0], 2, second[1], nc.scalar.copy)
+            if n > 0:
+                quant_y(rounds[n - 1][1][0], 2, 1)
+            if n + 3 < 6:
+                product_upper(n + 3)
+            quant_y(first[0], 2, first[1])
+        group_y(10, 2, 0, nc.vector.tensor_copy)
+        turn_y(10, 1, 1)
+        turn_y(11, 1, 1)
+        group_y(10, 1, 1, nc.scalar.copy)
+        quant_y(10, 2, 0)
+        group_y(11, 1, 1, nc.vector.tensor_copy)
+        quant_y(10, 1, 1)
+        quant_y(11, 1, 1)
+
+        store_y(0, 2, 0, S)
+        store_y(2, 4, 0, S)
+        store_codes(0, 2, 0, 512)
+        store_y(4, 6, 0, S)
+        store_y(6, 8, 0, S)
+        store_scales(0, 1024, [nc.sync] * 4)
+        store_codes(0, 2, 512, 1024)
+        store_y(8, 10, 0, S)
+        store_y(10, 12, 0, HALF)
+        store_y(10, 11, HALF, S)
+        store_y(11, 12, HALF, S)
+        store_codes(0, 1, 1024, 1536)
+        store_codes(1, 2, 1024, 1536)
+        store_scales(1024, 1536, [nc.scalar] * 4)

@@ -183,13 +183,13 @@ def tile_softcap_logit_gradient_k2_kernel(
         nc.vector.memset(g_scl[:].rearrange("p g n -> p (g n)").bitcast(I32), 0)
         nc.vector.memset(delta_rows[:], 0.0)
         make_identity(nc, ident_f[:])
-        for r in range(4):
-            nc.gpsimd.dma_start(out=g_scl[r:P:32].bitcast(I32), in_=g_scales_v[r].bitcast(I32))
-        nc.gpsimd.dma_start(out=delta_rows[0:N_TILES, :], in_=delta.rearrange("(i p) -> i p", p=P))
         nc.vector.tensor_copy(out=ident_b[:], in_=ident_f[:])
 
         load_v(0)
         load_v(1)
+        for r in range(4):
+            nc.sync.dma_start(out=g_scl[r:P:32].bitcast(I32), in_=g_scales_v[r].bitcast(I32))
+        nc.sync.dma_start(out=delta_rows[0:N_TILES, :], in_=delta.rearrange("(i p) -> i p", p=P))
         load_ws(0, 1)
         load_g(0, 256)
         load_ws(1, 2)

@@ -17,8 +17,12 @@ ALU = mybir.AluOpType
 
 P = 128
 HALF = 512
+GROUP_WORDS = 256
 N_TILES = T // P
+N_PAIRS = N_TILES // 2
 V_KEYS = 256
+G_FIRST = 512
+EARLY_QUERIES = 768
 
 
 def tile_softcap_logit_gradient_k2_kernel(
@@ -27,9 +31,9 @@ def tile_softcap_logit_gradient_k2_kernel(
     nc = tc.nc
     with ExitStack() as ctx:
         keep = ctx.enter_context(tc.tile_pool(name="keep", bufs=1))
-        ws_pool = ctx.enter_context(tc.tile_pool(name="ws_pool", bufs=2))
+        ws_pool = ctx.enter_context(tc.tile_pool(name="ws_pool", bufs=4))
         ybf_pool = ctx.enter_context(tc.tile_pool(name="ybf_pool", bufs=4))
-        grp_pool = ctx.enter_context(tc.tile_pool(name="grp_pool", bufs=3))
+        grp_pool = ctx.enter_context(tc.tile_pool(name="grp_pool", bufs=4))
         acc_pool = ctx.enter_context(tc.psum_pool(name="acc_pool", bufs=4))
         turn_pool = ctx.enter_context(tc.psum_pool(name="turn_pool", bufs=4))
         ctx.enter_context(tc.manual_schedule())
@@ -39,7 +43,7 @@ def tile_softcap_logit_gradient_k2_kernel(
         delta_rows = keep.tile([P, P], BF16, name="delta_rows")
         delta_col = keep.tile([P, N_TILES], F32, name="delta_col")
         v_raw = keep.tile([P, 4, 2, D], BF16, name="v_raw", align_bytes=64)
-        v_grp = keep.tile([P, 4, 2, V_KEYS * 4], BF16, name="v_grp", align_bytes=64)
+        v_grp = keep.tile([P, 4, 2, V_KEYS * 2], F32, name="v_grp", align_bytes=64)
         v_codes = keep.tile([P, 2, S], U32, name="v_codes", align_bytes=64)
         v_scl = keep.tile([P, 2, S], U8, name="v_scl", align_bytes=64)
         g_codes = keep.tile([P, 2, T], U32, name="g_codes", align_bytes=64)
@@ -49,6 +53,7 @@ def tile_softcap_logit_gradient_k2_kernel(
         y_sb = keep.tile([P, N_TILES, S], F32, name="y_sb", align_bytes=64)
         y_codes = keep.tile([P, 2, T], U32, name="y_codes", align_bytes=64)
         y_scl = keep.tile([P, 2, T], U8, name="y_scl", align_bytes=64)
+        shared = [keep.tile([P, 2, HALF], F32, name="shared%d" % r, align_bytes=64) for r in range(2)]
 
         g_words_v = g_words.rearrange("g p n t -> p g (n t)")
         out_words_v = out_1.rearrange("g p n t -> p g (n t)")
@@ -58,9 +63,7 @@ def tile_softcap_logit_gradient_k2_kernel(
         s_v = slope.rearrange("(i p) s -> p i s", p=P)
         y_v = out_0.rearrange("(i p) s -> p i s", p=P)
 
-        ws_head = keep.tile([P, 4, S], F32, name="ws_head", align_bytes=64)
-        shared = [keep.tile([P, 2, HALF], F32, name="shared%d" % r, align_bytes=64) for r in range(2)]
-        ws, acc, ybf, grp, ybank = {}, {}, {}, {}, {}
+        ws, acc, ybf, y_bank, y_grp, v_bank = {}, {}, {}, {}, {}, {}
 
         def load_v(c):
             rows = v[c * V_KEYS : (c + 1) * V_KEYS, :]
@@ -76,26 +79,32 @@ def tile_softcap_logit_gradient_k2_kernel(
             nc.sync.dma_start(out=s_sb[:, i0:i1], in_=s_v[:, i0:i1])
 
         def turn_v(c, g):
-            bank = turn_pool.tile([P, 2, 2, P], F32, name="bank")
+            v_bank[c, g] = turn_pool.tile([P, 2, 2, P], F32, name="bank")
             for j in range(2):
                 words = v_raw[:, c, j, :].bitcast(F32)
                 for u in range(2):
-                    nc.tensor.transpose(bank[:, j, u, :], words[:, 256 * g + u : 256 * (g + 1) : 2], ident_f[:])
-            nc.scalar.copy(
-                out=v_grp[:, c, g, :].bitcast(F32).rearrange("k (m j u) -> k m j u", j=2, u=2),
-                in_=bank[:].rearrange("k j u m -> k m j u"),
+                    every_2nd = words[:, GROUP_WORDS * g + u : GROUP_WORDS * (g + 1) : 2]
+                    nc.tensor.transpose(v_bank[c, g][:, j, u, :], every_2nd, ident_f[:])
+
+        def group_v(c, g, copy):
+            copy(
+                out=v_grp[:, c, g, :].rearrange("k (m j u) -> k m j u", j=2, u=2),
+                in_=v_bank[c, g][:].rearrange("k j u m -> k m j u"),
             )
 
         def quant_v(c, g):
             keys = slice(c * V_KEYS, (c + 1) * V_KEYS)
             nc.vector.quantize_mx(
-                out=v_codes[:, g, keys].bitcast(E4M3X4), scales=v_scl[:, g, keys], in_=v_grp[:, c, g, :]
+                out=v_codes[:, g, keys].bitcast(E4M3X4), scales=v_scl[:, g, keys], in_=v_grp[:, c, g, :].bitcast(BF16)
             )
 
         def product_tile(i):
-            nc.vector.tensor_tensor(out=ws_head[:, i, :], in0=w_sb[:, i, :], in1=s_sb[:, i, :], op=ALU.mult)
+            dst = ws_pool.tile([P, 2, HALF], F32, name="ws")
+            nc.vector.tensor_tensor(
+                out=dst[:].rearrange("q h k -> q (h k)"), in0=w_sb[:, i, :], in1=s_sb[:, i, :], op=ALU.mult
+            )
             for h in range(2):
-                ws[i, h] = ws_head[:, i, h * HALF : (h + 1) * HALF]
+                ws[i, h] = dst[:, h, :]
 
         def product_pair(engine, dst, pair, h):
             tiles = slice(2 * pair, 2 * pair + 2)
@@ -104,66 +113,72 @@ def tile_softcap_logit_gradient_k2_kernel(
             for a in range(2):
                 ws[2 * pair + a, h] = dst[:, a, :]
 
-        def product_upper(pair):
-            dst = ws_pool.tile([P, 2, HALF], F32, name="ws")
-            product_pair(nc.vector, dst, pair, 1)
-
         def product_lower(pair):
-            product_pair(nc.gpsimd, shared[pair % 2], pair, 0)
+            dst = ws_pool.tile([P, 2, HALF], F32, name="ws")
+            product_pair(nc.vector, dst, pair, 0)
 
-        def matmul(i, h):
-            acc[i, h] = acc_pool.tile([P, HALF], F32, name="acc")
-            queries = slice(i * P, (i + 1) * P)
+        def matmul_pair(i0, h):
             keys = slice(h * HALF, (h + 1) * HALF)
-            for g in range(2):
-                nc.tensor.matmul_mx(
-                    out=acc[i, h][:],
-                    lhsT=g_codes[:, g, queries].bitcast(E5M2X4),
-                    lhsT_scale=g_scl[:, g, queries],
-                    rhs=v_codes[:, g, keys].bitcast(E4M3X4),
-                    rhs_scale=v_scl[:, g, keys],
-                    start=(g == 0),
-                    stop=(g == 1),
-                )
+            for i in (i0, i0 + 1):
+                acc[i, h] = acc_pool.tile([P, HALF], F32, name="acc")
+                queries = slice(i * P, (i + 1) * P)
+                for g in range(2):
+                    nc.tensor.matmul_mx(
+                        out=acc[i, h][:],
+                        lhsT=g_codes[:, g, queries].bitcast(E5M2X4),
+                        lhsT_scale=g_scl[:, g, queries],
+                        rhs=v_codes[:, g, keys].bitcast(E4M3X4),
+                        rhs_scale=v_scl[:, g, keys],
+                        start=(g == 0),
+                        stop=(g == 1),
+                    )
 
         def gradient(i, h):
-            keys = slice(h * HALF, (h + 1) * HALF)
             nc.vector.scalar_tensor_tensor(
-                out=y_sb[:, i, keys],
+                out=y_sb[:, i, h * HALF : (h + 1) * HALF],
                 in0=acc[i, h][:],
                 scalar=delta_col[:, i : i + 1],
                 in1=ws[i, h],
                 op0=ALU.subtract,
                 op1=ALU.mult,
             )
+
+        def round_y(i, h):
             ybf[i, h] = ybf_pool.tile([P, 2, P, 2], BF16, name="ybf")
             nc.scalar.copy(
-                out=ybf[i, h][:], in_=y_sb[:, i, keys].rearrange("q (p u e) -> q u p e", u=2, e=2)
+                out=ybf[i, h][:],
+                in_=y_sb[:, i, h * HALF : (h + 1) * HALF].rearrange("q (p u e) -> q u p e", u=2, e=2),
             )
 
+        def gradient_pair(i0, h):
+            for i in (i0, i0 + 1):
+                gradient(i, h)
+                round_y(i, h)
+
         def turn_y(i0, n, h):
-            ybank[i0, h] = turn_pool.tile([P, n, 2, P], F32, name="bank")
+            y_bank[i0, h] = turn_pool.tile([P, n, 2, P], F32, name="bank")
             for a in range(n):
                 for u in range(2):
                     words = ybf[i0 + a, h][:, u].rearrange("q p e -> q (p e)").bitcast(F32)
-                    nc.tensor.transpose(ybank[i0, h][:, a, u, :], words, ident_f[:])
+                    nc.tensor.transpose(y_bank[i0, h][:, a, u, :], words, ident_f[:])
 
-        def group_y(i0, n, h, copy, home=None):
-            if home is None:
-                tile = grp_pool.tile([P, n * P * 2], F32, name="grp", align_bytes=64)
-                home = tile[:]
-            grp[i0, h] = home
+        def group_y_into(dst, i0, n, h, copy):
+            y_grp[i0, h] = dst
             copy(
-                out=home.rearrange("k (a m u) -> k a m u", a=n, u=2),
-                in_=ybank[i0, h][:].rearrange("k a u m -> k a m u"),
+                out=dst.rearrange("k (a m u) -> k a m u", a=n, u=2),
+                in_=y_bank[i0, h][:].rearrange("k a u m -> k a m u"),
             )
+
+        def group_y(i0, n, h, copy):
+            dst = grp_pool.tile([P, n * P * 2], F32, name="grp", align_bytes=64)
+            group_y_into(dst[:], i0, n, h, copy)
 
         def quant_y(i0, n, h):
             queries = slice(i0 * P, (i0 + n) * P)
             nc.vector.quantize_mx(
                 out=y_codes[:, h, queries].bitcast(E4M3X4),
                 scales=y_scl[:, h, queries],
-                in_=grp[i0, h].bitcast(BF16),
+                in_=y_grp[i0, h].bitcast(BF16),
             )
 
         def store_y(i0, i1, k0, k1):
@@ -174,9 +189,9 @@ def tile_softcap_logit_gradient_k2_kernel(
                 out=out_words_v[:, h0:h1, 4 * n0 : 4 * n1].bitcast(I32), in_=y_codes[:, h0:h1, n0:n1].bitcast(I32)
             )
 
-        def store_scales(n0, n1, queues):
+        def store_scales(queue, n0, n1):
             for r in range(4):
-                queues[r].dma_start(
+                queue.dma_start(
                     out=out_scales_v[r][:, :, n0:n1].bitcast(I32), in_=y_scl[r:P:32, :, n0:n1].bitcast(I32)
                 )
 
@@ -187,113 +202,94 @@ def tile_softcap_logit_gradient_k2_kernel(
 
         load_v(0)
         load_v(1)
+        load_ws(0, 1)
+        load_g(0, G_FIRST)
         for r in range(4):
             nc.sync.dma_start(out=g_scl[r:P:32].bitcast(I32), in_=g_scales_v[r].bitcast(I32))
         nc.sync.dma_start(out=delta_rows[0:N_TILES, :], in_=delta.rearrange("(i p) -> i p", p=P))
-        load_ws(0, 1)
-        load_g(0, 256)
         load_ws(1, 2)
-        load_ws(2, 3)
-        load_g(256, 512)
         load_v(2)
-        load_ws(3, 4)
         load_v(3)
+        load_ws(2, 4)
         load_ws(4, 6)
-        load_g(512, 1024)
-        load_ws(6, 8)
-        load_g(1024, 1536)
-        load_ws(8, 10)
-        load_ws(10, 12)
+        load_g(G_FIRST, T)
+        for pair in range(3, N_PAIRS):
+            load_ws(2 * pair, 2 * pair + 2)
 
-        turn_v(0, 0)
-        turn_v(0, 1)
-        turn_v(1, 0)
-        turn_v(1, 1)
+        for c in range(2):
+            for g in range(2):
+                turn_v(c, g)
+                group_v(c, g, nc.scalar.copy)
+        quant_v(0, 0)
+        product_tile(0)
+        quant_v(0, 1)
+        quant_v(1, 0)
+        quant_v(1, 1)
         delta_bank = turn_pool.tile([P, P], BF16, name="bank")
         nc.tensor.transpose(delta_bank[:], delta_rows[:], ident_b[:])
         nc.scalar.copy(out=delta_col[:], in_=delta_bank[:, 0:N_TILES])
-        quant_v(0, 0)
-        quant_v(0, 1)
-        product_tile(0)
-        quant_v(1, 0)
-        quant_v(1, 1)
-        for i in range(4):
-            matmul(i, 0)
+        matmul_pair(0, 0)
         product_tile(1)
         gradient(0, 0)
         gradient(1, 0)
-        turn_v(2, 0)
-        turn_v(2, 1)
+
+        for c in range(2, 4):
+            round_y(c - 2, 0)
+            turn_v(c, 0)
+            turn_v(c, 1)
+            group_v(c, 0, nc.scalar.copy)
+            group_v(c, 1, nc.vector.tensor_copy)
+            quant_v(c, 0)
+            quant_v(c, 1)
         turn_y(0, 2, 0)
-        group_y(0, 2, 0, nc.scalar.copy)
-        product_tile(2)
-        gradient(2, 0)
-        product_tile(3)
-        quant_v(2, 0)
-        quant_v(2, 1)
-        turn_v(3, 0)
-        turn_v(3, 1)
-        gradient(3, 0)
+        group_y_into(shared[0][:, 0, :], 0, 2, 0, nc.scalar.copy)
+        matmul_pair(2, 0)
+        matmul_pair(0, 1)
+        product_lower(1)
         quant_y(0, 2, 0)
-        quant_v(3, 0)
-        quant_v(3, 1)
-        turn_y(2, 2, 0)
-        matmul(0, 1)
-        matmul(1, 1)
-        matmul(2, 1)
-        matmul(3, 1)
-        group_y(2, 2, 0, nc.scalar.copy, shared[0][:, 0, :])
-        product_upper(2)
-        quant_y(2, 2, 0)
 
-        rounds = [[(0, 1), (2, 1)]] + [[(i0, 0), (i0, 1)] for i0 in range(4, N_TILES, 2)]
-        for n, (first, second) in enumerate(rounds):
-            last = n + 1 == len(rounds)
-            nxt = None if last else rounds[n + 1]
-            if not last:
-                product_lower(n + 2)
-            gradient(first[0], first[1])
-            gradient(first[0] + 1, first[1])
-            if last:
-                quant_y(rounds[n - 1][1][0], 2, 1)
-            if not last:
-                matmul(nxt[0][0], nxt[0][1])
-                matmul(nxt[0][0] + 1, nxt[0][1])
-            turn_y(first[0], 2, first[1])
-            gradient(second[0], second[1])
-            gradient(second[0] + 1, second[1])
-            if last:
-                break
-            matmul(nxt[1][0], nxt[1][1])
-            matmul(nxt[1][0] + 1, nxt[1][1])
-            turn_y(second[0], 2, second[1])
-            group_y(first[0], 2, first[1], nc.scalar.copy, shared[(n + 1) % 2][:, 0, :] if n + 3 < 6 else None)
-            group_y(second[0], 2, second[1], nc.scalar.copy)
-            if n > 0:
-                quant_y(rounds[n - 1][1][0], 2, 1)
-            if n + 3 < 6:
-                product_upper(n + 3)
-            quant_y(first[0], 2, first[1])
-        group_y(10, 2, 0, nc.vector.tensor_copy)
-        turn_y(10, 1, 1)
-        turn_y(11, 1, 1)
-        group_y(10, 1, 1, nc.scalar.copy)
-        quant_y(10, 2, 0)
-        group_y(11, 1, 1, nc.vector.tensor_copy)
-        quant_y(10, 1, 1)
-        quant_y(11, 1, 1)
+        last_pair = N_PAIRS - 1
+        for pair in range(last_pair):
+            i0 = 2 * pair
+            more_rounds = pair + 1 < last_pair
+            product_pair(nc.gpsimd, shared[pair % 2], pair + 1, 1)
+            gradient_pair(i0, 1)
+            matmul_pair(i0 + 2, 1)
+            turn_y(i0, 2, 1)
+            gradient_pair(i0 + 2, 0)
+            if more_rounds:
+                matmul_pair(i0 + 4, 0)
+            turn_y(i0 + 2, 2, 0)
+            if more_rounds:
+                group_y_into(shared[(pair + 1) % 2][:, 0, :], i0, 2, 1, nc.scalar.copy)
+                group_y(i0 + 2, 2, 0, nc.scalar.copy)
+                if pair > 0:
+                    quant_y(i0, 2, 0)
+                product_lower(pair + 2)
+                quant_y(i0, 2, 1)
 
-        store_y(0, 2, 0, S)
-        store_y(2, 4, 0, S)
-        store_codes(0, 2, 0, 512)
+        i_last = 2 * last_pair
+        group_y(i_last - 2, 2, 1, nc.scalar.copy)
+        gradient_pair(i_last, 1)
+        quant_y(i_last - 2, 2, 0)
+        group_y(i_last, 2, 0, nc.vector.tensor_copy)
+        quant_y(i_last - 2, 2, 1)
+        for i in (i_last, i_last + 1):
+            turn_y(i, 1, 1)
+        for i in (i_last, i_last + 1):
+            group_y(i, 1, 1, nc.scalar.copy)
+        quant_y(i_last, 2, 0)
+        for i in (i_last, i_last + 1):
+            quant_y(i, 1, 1)
+
+        store_y(0, 4, 0, S)
         store_y(4, 6, 0, S)
+        store_codes(0, 2, 0, EARLY_QUERIES)
         store_y(6, 8, 0, S)
-        store_scales(0, 1024, [nc.sync] * 4)
-        store_codes(0, 2, 512, 1024)
+        store_scales(nc.sync, 0, EARLY_QUERIES)
         store_y(8, 10, 0, S)
-        store_y(10, 12, 0, HALF)
-        store_y(10, 11, HALF, S)
-        store_y(11, 12, HALF, S)
-        store_codes(0, 1, 1024, 1536)
-        store_codes(1, 2, 1024, 1536)
-        store_scales(1024, 1536, [nc.scalar] * 4)
+        store_y(i_last, N_TILES, 0, HALF)
+        store_y(i_last, N_TILES, HALF, S)
+        store_codes(0, 1, EARLY_QUERIES, T)
+        store_codes(1, 2, EARLY_QUERIES, T)
+        store_scales(nc.scalar, EARLY_QUERIES, T)

from contextlib import ExitStack

import concourse.mybir as mybir
from concourse.masks import make_identity

T, S, D = 1536, 1024, 1024
FLOPS = 2 * T * S * D

F32 = mybir.dt.float32
BF16 = mybir.dt.bfloat16
I32 = mybir.dt.int32
U32 = mybir.dt.uint32
U8 = mybir.dt.uint8
E4M3X4 = mybir.dt.float8_e4m3fn_x4
E5M2X4 = mybir.dt.float8_e5m2_x4
ALU = mybir.AluOpType

P = 128
HALF = 512
GROUP_WORDS = 256
N_TILES = T // P
N_PAIRS = N_TILES // 2
V_KEYS = 256
G_FIRST = 512
EARLY_QUERIES = 768


def tile_softcap_logit_gradient_k2_kernel(
    tc, g_words, g_scales, v, weights, slope, delta, out_0, out_1, out_2
):
    nc = tc.nc
    with ExitStack() as ctx:
        keep = ctx.enter_context(tc.tile_pool(name="keep", bufs=1))
        ws_pool = ctx.enter_context(tc.tile_pool(name="ws_pool", bufs=4))
        ybf_pool = ctx.enter_context(tc.tile_pool(name="ybf_pool", bufs=4))
        grp_pool = ctx.enter_context(tc.tile_pool(name="grp_pool", bufs=4))
        acc_pool = ctx.enter_context(tc.psum_pool(name="acc_pool", bufs=4))
        turn_pool = ctx.enter_context(tc.psum_pool(name="turn_pool", bufs=4))
        ctx.enter_context(tc.manual_schedule())

        ident_f = keep.tile([P, P], F32, name="ident_f")
        ident_b = keep.tile([P, P], BF16, name="ident_b")
        delta_rows = keep.tile([P, P], BF16, name="delta_rows")
        delta_col = keep.tile([P, N_TILES], F32, name="delta_col")
        v_raw = keep.tile([P, 4, 2, D], BF16, name="v_raw", align_bytes=64)
        v_grp = keep.tile([P, 4, 2, V_KEYS * 2], F32, name="v_grp", align_bytes=64)
        v_codes = keep.tile([P, 2, S], U32, name="v_codes", align_bytes=64)
        v_scl = keep.tile([P, 2, S], U8, name="v_scl", align_bytes=64)
        g_codes = keep.tile([P, 2, T], U32, name="g_codes", align_bytes=64)
        g_scl = keep.tile([P, 2, T], U8, name="g_scl", align_bytes=64)
        w_sb = keep.tile([P, N_TILES, S], BF16, name="w_sb", align_bytes=64)
        s_sb = keep.tile([P, N_TILES, S], BF16, name="s_sb", align_bytes=64)
        y_sb = keep.tile([P, N_TILES, S], F32, name="y_sb", align_bytes=64)
        y_codes = keep.tile([P, 2, T], U32, name="y_codes", align_bytes=64)
        y_scl = keep.tile([P, 2, T], U8, name="y_scl", align_bytes=64)
        shared = [keep.tile([P, 2, HALF], F32, name="shared%d" % r, align_bytes=64) for r in range(2)]

        g_words_v = g_words.rearrange("g p n t -> p g (n t)")
        out_words_v = out_1.rearrange("g p n t -> p g (n t)")
        g_scales_v = g_scales.rearrange("g (q r) n -> r q g n", r=4)
        out_scales_v = out_2.rearrange("g (q r) n -> r q g n", r=4)
        w_v = weights.rearrange("(i p) s -> p i s", p=P)
        s_v = slope.rearrange("(i p) s -> p i s", p=P)
        y_v = out_0.rearrange("(i p) s -> p i s", p=P)

        ws, acc, ybf, y_bank, y_grp, v_bank = {}, {}, {}, {}, {}, {}

        def load_v(c):
            rows = v[c * V_KEYS : (c + 1) * V_KEYS, :]
            nc.sync.dma_start(out=v_raw[:, c], in_=rows.rearrange("(p j) d -> p j d", j=2))

        def load_g(n0, n1):
            nc.sync.dma_start(
                out=g_codes[:, :, n0:n1].bitcast(I32), in_=g_words_v[:, :, 4 * n0 : 4 * n1].bitcast(I32)
            )

        def load_ws(i0, i1):
            nc.sync.dma_start(out=w_sb[:, i0:i1], in_=w_v[:, i0:i1])
            nc.sync.dma_start(out=s_sb[:, i0:i1], in_=s_v[:, i0:i1])

        def turn_v(c, g):
            v_bank[c, g] = turn_pool.tile([P, 2, 2, P], F32, name="bank")
            for j in range(2):
                words = v_raw[:, c, j, :].bitcast(F32)
                for u in range(2):
                    every_2nd = words[:, GROUP_WORDS * g + u : GROUP_WORDS * (g + 1) : 2]
                    nc.tensor.transpose(v_bank[c, g][:, j, u, :], every_2nd, ident_f[:])

        def group_v(c, g, copy):
            copy(
                out=v_grp[:, c, g, :].rearrange("k (m j u) -> k m j u", j=2, u=2),
                in_=v_bank[c, g][:].rearrange("k j u m -> k m j u"),
            )

        def quant_v(c, g):
            keys = slice(c * V_KEYS, (c + 1) * V_KEYS)
            nc.vector.quantize_mx(
                out=v_codes[:, g, keys].bitcast(E4M3X4), scales=v_scl[:, g, keys], in_=v_grp[:, c, g, :].bitcast(BF16)
            )

        def product_tile(i):
            dst = ws_pool.tile([P, 2, HALF], F32, name="ws")
            nc.vector.tensor_tensor(
                out=dst[:].rearrange("q h k -> q (h k)"), in0=w_sb[:, i, :], in1=s_sb[:, i, :], op=ALU.mult
            )
            for h in range(2):
                ws[i, h] = dst[:, h, :]

        def product_pair(engine, dst, pair, h):
            tiles = slice(2 * pair, 2 * pair + 2)
            keys = slice(h * HALF, (h + 1) * HALF)
            engine.tensor_tensor(out=dst[:], in0=w_sb[:, tiles, keys], in1=s_sb[:, tiles, keys], op=ALU.mult)
            for a in range(2):
                ws[2 * pair + a, h] = dst[:, a, :]

        def product_lower(pair):
            dst = ws_pool.tile([P, 2, HALF], F32, name="ws")
            product_pair(nc.vector, dst, pair, 0)

        def matmul_pair(i0, h):
            keys = slice(h * HALF, (h + 1) * HALF)
            for i in (i0, i0 + 1):
                acc[i, h] = acc_pool.tile([P, HALF], F32, name="acc")
                queries = slice(i * P, (i + 1) * P)
                for g in range(2):
                    nc.tensor.matmul_mx(
                        out=acc[i, h][:],
                        lhsT=g_codes[:, g, queries].bitcast(E5M2X4),
                        lhsT_scale=g_scl[:, g, queries],
                        rhs=v_codes[:, g, keys].bitcast(E4M3X4),
                        rhs_scale=v_scl[:, g, keys],
                        start=(g == 0),
                        stop=(g == 1),
                    )

        def gradient(i, h):
            nc.vector.scalar_tensor_tensor(
                out=y_sb[:, i, h * HALF : (h + 1) * HALF],
                in0=acc[i, h][:],
                scalar=delta_col[:, i : i + 1],
                in1=ws[i, h],
                op0=ALU.subtract,
                op1=ALU.mult,
            )

        def round_y(i, h):
            ybf[i, h] = ybf_pool.tile([P, 2, P, 2], BF16, name="ybf")
            nc.scalar.copy(
                out=ybf[i, h][:],
                in_=y_sb[:, i, h * HALF : (h + 1) * HALF].rearrange("q (p u e) -> q u p e", u=2, e=2),
            )

        def gradient_pair(i0, h):
            for i in (i0, i0 + 1):
                gradient(i, h)
                round_y(i, h)

        def turn_y(i0, n, h):
            y_bank[i0, h] = turn_pool.tile([P, n, 2, P], F32, name="bank")
            for a in range(n):
                for u in range(2):
                    words = ybf[i0 + a, h][:, u].rearrange("q p e -> q (p e)").bitcast(F32)
                    nc.tensor.transpose(y_bank[i0, h][:, a, u, :], words, ident_f[:])

        def group_y_into(dst, i0, n, h, copy):
            y_grp[i0, h] = dst
            copy(
                out=dst.rearrange("k (a m u) -> k a m u", a=n, u=2),
                in_=y_bank[i0, h][:].rearrange("k a u m -> k a m u"),
            )

        def group_y(i0, n, h, copy):
            dst = grp_pool.tile([P, n * P * 2], F32, name="grp", align_bytes=64)
            group_y_into(dst[:], i0, n, h, copy)

        def quant_y(i0, n, h):
            queries = slice(i0 * P, (i0 + n) * P)
            nc.vector.quantize_mx(
                out=y_codes[:, h, queries].bitcast(E4M3X4),
                scales=y_scl[:, h, queries],
                in_=y_grp[i0, h].bitcast(BF16),
            )

        def store_y(i0, i1, k0, k1):
            nc.sync.dma_start(out=y_v[:, i0:i1, k0:k1], in_=y_sb[:, i0:i1, k0:k1])

        def store_codes(h0, h1, n0, n1):
            nc.sync.dma_start(
                out=out_words_v[:, h0:h1, 4 * n0 : 4 * n1].bitcast(I32), in_=y_codes[:, h0:h1, n0:n1].bitcast(I32)
            )

        def store_scales(queue, n0, n1):
            for r in range(4):
                queue.dma_start(
                    out=out_scales_v[r][:, :, n0:n1].bitcast(I32), in_=y_scl[r:P:32, :, n0:n1].bitcast(I32)
                )

        nc.vector.memset(g_scl[:].rearrange("p g n -> p (g n)").bitcast(I32), 0)
        nc.vector.memset(delta_rows[:], 0.0)
        make_identity(nc, ident_f[:])
        nc.vector.tensor_copy(out=ident_b[:], in_=ident_f[:])

        load_v(0)
        load_v(1)
        load_ws(0, 1)
        load_g(0, G_FIRST)
        for r in range(4):
            nc.sync.dma_start(out=g_scl[r:P:32].bitcast(I32), in_=g_scales_v[r].bitcast(I32))
        nc.sync.dma_start(out=delta_rows[0:N_TILES, :], in_=delta.rearrange("(i p) -> i p", p=P))
        load_ws(1, 2)
        load_v(2)
        load_v(3)
        load_ws(2, 4)
        load_ws(4, 6)
        load_g(G_FIRST, T)
        for pair in range(3, N_PAIRS):
            load_ws(2 * pair, 2 * pair + 2)

        for c in range(2):
            for g in range(2):
                turn_v(c, g)
                group_v(c, g, nc.scalar.copy)
        quant_v(0, 0)
        product_tile(0)
        quant_v(0, 1)
        quant_v(1, 0)
        quant_v(1, 1)
        delta_bank = turn_pool.tile([P, P], BF16, name="bank")
        nc.tensor.transpose(delta_bank[:], delta_rows[:], ident_b[:])
        nc.scalar.copy(out=delta_col[:], in_=delta_bank[:, 0:N_TILES])
        matmul_pair(0, 0)
        product_tile(1)
        gradient(0, 0)
        gradient(1, 0)

        for c in range(2, 4):
            round_y(c - 2, 0)
            turn_v(c, 0)
            turn_v(c, 1)
            group_v(c, 0, nc.scalar.copy)
            group_v(c, 1, nc.vector.tensor_copy)
            quant_v(c, 0)
            quant_v(c, 1)
        turn_y(0, 2, 0)
        group_y_into(shared[0][:, 0, :], 0, 2, 0, nc.scalar.copy)
        matmul_pair(2, 0)
        matmul_pair(0, 1)
        product_lower(1)
        quant_y(0, 2, 0)

        last_pair = N_PAIRS - 1
        for pair in range(last_pair):
            i0 = 2 * pair
            more_rounds = pair + 1 < last_pair
            product_pair(nc.gpsimd, shared[pair % 2], pair + 1, 1)
            gradient_pair(i0, 1)
            matmul_pair(i0 + 2, 1)
            turn_y(i0, 2, 1)
            gradient_pair(i0 + 2, 0)
            if more_rounds:
                matmul_pair(i0 + 4, 0)
            turn_y(i0 + 2, 2, 0)
            if more_rounds:
                group_y_into(shared[(pair + 1) % 2][:, 0, :], i0, 2, 1, nc.scalar.copy)
                group_y(i0 + 2, 2, 0, nc.scalar.copy)
                if pair > 0:
                    quant_y(i0, 2, 0)
                product_lower(pair + 2)
                quant_y(i0, 2, 1)

        i_last = 2 * last_pair
        group_y(i_last - 2, 2, 1, nc.scalar.copy)
        gradient_pair(i_last, 1)
        quant_y(i_last - 2, 2, 0)
        group_y(i_last, 2, 0, nc.vector.tensor_copy)
        quant_y(i_last - 2, 2, 1)
        for i in (i_last, i_last + 1):
            turn_y(i, 1, 1)
        for i in (i_last, i_last + 1):
            group_y(i, 1, 1, nc.scalar.copy)
        quant_y(i_last, 2, 0)
        for i in (i_last, i_last + 1):
            quant_y(i, 1, 1)

        store_y(0, 4, 0, S)
        store_y(4, 6, 0, S)
        store_codes(0, 2, 0, EARLY_QUERIES)
        store_y(6, 8, 0, S)
        store_scales(nc.sync, 0, EARLY_QUERIES)
        store_y(8, 10, 0, S)
        store_y(i_last, N_TILES, 0, HALF)
        store_y(i_last, N_TILES, HALF, S)
        store_codes(0, 1, EARLY_QUERIES, T)
        store_codes(1, 2, EARLY_QUERIES, T)
        store_scales(nc.scalar, EARLY_QUERIES, T)
